import numpy as np
import ml_dtypes

BF16 = ml_dtypes.bfloat16


def bf(x):
    return np.asarray(x, np.float32).astype(BF16)


def f32(x):
    return np.asarray(x, np.float32)


def f64(x):
    return np.asarray(x).astype(np.float64)


def striped(idx):
    return np.tile(idx.reshape(-1, 16).T, (8, 1))


def rows(idx, k):
    return np.tile(idx, (k, 1))


def look(tab, idx):
    return np.take_along_axis(f64(tab), rows(idx, len(tab)), axis=1)


K, S, V, N = 128, 2048, 2048, 2048


def setup_inputs():
    return {"tab": f32(np.random.standard_normal((2, K, S))), "th": f32(0.5 * np.random.standard_normal((K, V))), "offs": striped(np.random.permutation(S)[:N])}


def reference(tab, th, offs):
    idx = offs[:16].T.reshape(-1)
    x = (look(tab[0], idx) >= f64(th)) * look(tab[1], idx)
    return x

@@ -1,0 +1,47 @@
+import concourse.mybir as mybir
+
+F32 = mybir.dt.float32
+U16 = mybir.dt.uint16
+is_ge = mybir.AluOpType.is_ge
+mult = mybir.AluOpType.mult
+
+ROWS = 128
+PLACES = 2048
+ENTRIES = 2048
+PIECE = 512
+COLUMN = 16
+
+
+def tile_lookup_sel_out_kernel(tc, tab, th, offs, out):
+    nc = tc.nc
+    pieces = ENTRIES // PIECE
+    with (
+        tc.tile_pool(name="held", bufs=1) as held,
+        tc.tile_pool(name="ring", bufs=pieces) as ring,
+    ):
+        offsets = held.tile([ROWS, ENTRIES // COLUMN], U16)
+        nc.sync.dma_start(offsets[:], offs)
+
+        keys = held.tile([ROWS, PLACES], F32)
+        nc.sync.dma_start(keys[:], tab[0])
+        thresholds = []
+        for p in range(pieces):
+            threshold = ring.tile([ROWS, PIECE], F32)
+            nc.sync.dma_start(threshold[:], th[:, p * PIECE : (p + 1) * PIECE])
+            thresholds.append(threshold)
+        values = held.tile([ROWS, PLACES], F32)
+        nc.sync.dma_start(values[:], tab[1])
+
+        def listed(p):
+            return offsets[:, p * PIECE // COLUMN : (p + 1) * PIECE // COLUMN]
+
+        reached_pieces = []
+        for p in range(pieces):
+            reached = ring.tile([ROWS, PIECE], F32)
+            nc.vector.tensor_tensor(reached[:], keys[:].indirect(listed(p)), thresholds[p][:], is_ge)
+            reached_pieces.append(reached)
+
+        for p in range(pieces):
+            picked = ring.tile([ROWS, PIECE], F32)
+            nc.vector.tensor_tensor(picked[:], values[:].indirect(listed(p)), reached_pieces[p][:], mult)
+            nc.scalar.dma_start(out[:, p * PIECE : (p + 1) * PIECE], picked[:])

@@ -8,40 +8,48 @@ mult = mybir.AluOpType.mult
 ROWS = 128
 PLACES = 2048
 ENTRIES = 2048
-PIECE = 512
 COLUMN = 16
+SHORTEST = 128
+
+
+def growing_pieces():
+    pieces = [(0, SHORTEST)]
+    while pieces[-1][1] < ENTRIES:
+        done = pieces[-1][1]
+        pieces.append((done, 2 * done))
+    return pieces
+
+
+def shrinking_pieces():
+    return [(ENTRIES - stop, ENTRIES - start) for start, stop in reversed(growing_pieces())]
 
 
 def tile_lookup_sel_out_kernel(tc, tab, th, offs, out):
     nc = tc.nc
-    pieces = ENTRIES // PIECE
-    with (
-        tc.tile_pool(name="held", bufs=1) as held,
-        tc.tile_pool(name="ring", bufs=pieces) as ring,
-    ):
+    with tc.tile_pool(name="held", bufs=1) as held:
         offsets = held.tile([ROWS, ENTRIES // COLUMN], U16)
-        nc.sync.dma_start(offsets[:], offs)
-
         keys = held.tile([ROWS, PLACES], F32)
-        nc.sync.dma_start(keys[:], tab[0])
-        thresholds = []
-        for p in range(pieces):
-            threshold = ring.tile([ROWS, PIECE], F32)
-            nc.sync.dma_start(threshold[:], th[:, p * PIECE : (p + 1) * PIECE])
-            thresholds.append(threshold)
         values = held.tile([ROWS, PLACES], F32)
+        thresholds = held.tile([ROWS, ENTRIES], F32)
+        reached = held.tile([ROWS, ENTRIES], F32)
+        picked = held.tile([ROWS, ENTRIES], F32)
+
+        nc.sync.dma_start(offsets[:], offs)
+        nc.sync.dma_start(keys[:], tab[0])
+        for start, stop in growing_pieces():
+            nc.sync.dma_start(thresholds[:, start:stop], th[:, start:stop])
         nc.sync.dma_start(values[:], tab[1])
 
-        def listed(p):
-            return offsets[:, p * PIECE // COLUMN : (p + 1) * PIECE // COLUMN]
+        def listed(start, stop):
+            return offsets[:, start // COLUMN : stop // COLUMN]
 
-        reached_pieces = []
-        for p in range(pieces):
-            reached = ring.tile([ROWS, PIECE], F32)
-            nc.vector.tensor_tensor(reached[:], keys[:].indirect(listed(p)), thresholds[p][:], is_ge)
-            reached_pieces.append(reached)
+        for start, stop in growing_pieces():
+            nc.vector.tensor_tensor(
+                reached[:, start:stop], keys[:].indirect(listed(start, stop)), thresholds[:, start:stop], is_ge
+            )
 
-        for p in range(pieces):
-            picked = ring.tile([ROWS, PIECE], F32)
-            nc.vector.tensor_tensor(picked[:], values[:].indirect(listed(p)), reached_pieces[p][:], mult)
-            nc.scalar.dma_start(out[:, p * PIECE : (p + 1) * PIECE], picked[:])
+        for start, stop in shrinking_pieces():
+            nc.vector.tensor_tensor(
+                picked[:, start:stop], values[:].indirect(listed(start, stop)), reached[:, start:stop], mult
+            )
+            nc.scalar.dma_start(out[:, start:stop], picked[:, start:stop])

@@ -35,7 +35,9 @@ def tile_lookup_sel_out_kernel(tc, tab, th, offs, out):
         picked = held.tile([ROWS, ENTRIES], F32)
 
         nc.sync.dma_start(offsets[:], offs)
-        nc.sync.dma_start(keys[:], tab[0])
+        half = PLACES // 2
+        nc.sync.dma_start(keys[:, :half], tab[0, :, :half])
+        nc.scalar.dma_start(keys[:, half:], tab[0, :, half:])
         for start, stop in growing_pieces():
             nc.sync.dma_start(thresholds[:, start:stop], th[:, start:stop])
         nc.sync.dma_start(values[:], tab[1])

import concourse.mybir as mybir

F32 = mybir.dt.float32
U16 = mybir.dt.uint16
is_ge = mybir.AluOpType.is_ge
mult = mybir.AluOpType.mult

ROWS = 128
PLACES = 2048
ENTRIES = 2048
COLUMN = 16
SHORTEST = 128


def growing_pieces():
    pieces = [(0, SHORTEST)]
    while pieces[-1][1] < ENTRIES:
        done = pieces[-1][1]
        pieces.append((done, 2 * done))
    return pieces


def shrinking_pieces():
    return [(ENTRIES - stop, ENTRIES - start) for start, stop in reversed(growing_pieces())]


def tile_lookup_sel_out_kernel(tc, tab, th, offs, out):
    nc = tc.nc
    with tc.tile_pool(name="held", bufs=1) as held:
        offsets = held.tile([ROWS, ENTRIES // COLUMN], U16)
        keys = held.tile([ROWS, PLACES], F32)
        values = held.tile([ROWS, PLACES], F32)
        thresholds = held.tile([ROWS, ENTRIES], F32)
        reached = held.tile([ROWS, ENTRIES], F32)
        picked = held.tile([ROWS, ENTRIES], F32)

        nc.sync.dma_start(offsets[:], offs)
        half = PLACES // 2
        nc.sync.dma_start(keys[:, :half], tab[0, :, :half])
        nc.scalar.dma_start(keys[:, half:], tab[0, :, half:])
        for start, stop in growing_pieces():
            nc.sync.dma_start(thresholds[:, start:stop], th[:, start:stop])
        nc.sync.dma_start(values[:], tab[1])

        def listed(start, stop):
            return offsets[:, start // COLUMN : stop // COLUMN]

        for start, stop in growing_pieces():
            nc.vector.tensor_tensor(
                reached[:, start:stop], keys[:].indirect(listed(start, stop)), thresholds[:, start:stop], is_ge
            )

        for start, stop in shrinking_pieces():
            nc.vector.tensor_tensor(
                picked[:, start:stop], values[:].indirect(listed(start, stop)), reached[:, start:stop], mult
            )
            nc.scalar.dma_start(out[:, start:stop], picked[:, start:stop])
